import numpy as np
import ml_dtypes


def mxq(x, axis, fmt="e4m3"):
    dtype, down = {"e4m3": (ml_dtypes.float8_e4m3fn, 7), "e5m2": (ml_dtypes.float8_e5m2, 14)}[fmt]
    v = np.moveaxis(np.asarray(x, np.float32).astype(ml_dtypes.bfloat16).astype(np.float64), axis, -1)
    blocks = v.reshape(v.shape[:-1] + (-1, 32))
    amax = np.abs(blocks).max(-1, keepdims=True)
    byte = np.maximum(np.where(amax > 0, np.frexp(amax)[1] - 1 + 127, 0) - down, 1)
    scale = np.exp2(byte - 127.0)
    codes = (blocks / scale).astype(np.float32).astype(dtype).astype(np.float64)
    return np.moveaxis((codes * scale).reshape(v.shape), -1, axis)


WIDE = False


def mx_kscale(k):
    if not WIDE:
        return np.ones(k)
    levels = np.array([10, -10, 5, -5, 0])
    if k % 512:
        return np.exp2(np.random.permutation(np.resize(levels, k // 32))).repeat(32)
    a = np.empty((k // 512, 16))
    for p in range(k // 512):
        a[p, :8] = np.random.permutation(np.resize(levels, 8))
        for g in range(8):
            far = levels[np.abs(levels - a[p, g]) >= 10]
            a[p, g + 8] = far[np.random.randint(len(far))]
    return np.exp2(a.ravel()).repeat(32)


def f64(x):
    return np.asarray(x).astype(np.float64)


def striped(idx):
    return np.tile(idx.reshape(-1, 16).T, (8, 1)).astype(np.uint16)


def unstriped(offs):
    return offs[:16].T.reshape(-1).astype(np.int64)


def striped8(idx):
    return np.concatenate([x.reshape(-1, 16).T for x in idx]).astype(np.uint16)


def runs(offs, k):
    lists = np.stack([offs[16 * r : 16 * r + 16].T.reshape(-1) for r in range(8)]).astype(np.int64)
    return lists[np.arange(k) % 512 // 64]


def pack_weight(w):
    k, n = w.shape
    w = f64(np.asarray(w, np.float32).astype(ml_dtypes.bfloat16)).reshape(k // 32, 32, n)
    amax = np.abs(w).max(1)
    byte = np.clip(np.where(amax > 0, np.frexp(amax)[1] - 1 + 127 - 7, 1), 1, 254)
    scaled = (w * np.exp2(127.0 - byte)[:, None, :]).reshape(k, n).astype(np.float32)
    words = np.ascontiguousarray(scaled.reshape(k // 512, 128, 4, n).transpose(0, 1, 3, 2)).astype(ml_dtypes.float8_e4m3fn).view(np.uint8)
    return words, np.ascontiguousarray(byte.astype(np.uint8).reshape(k // 512, 16, n))


def unpack_weight(words, scales):
    g, p, n, _ = words.shape
    vals = np.ascontiguousarray(words).view(ml_dtypes.float8_e4m3fn).astype(np.float64) * np.repeat(np.exp2(scales.astype(np.float64) - 127.0), 8, axis=1)[..., None]
    return vals.transpose(0, 1, 3, 2).reshape(g * 512, n)


def silu(v):
    return v / (1.0 + np.exp(-np.maximum(v, -700.0)))


K, T, S, V, N, H = 512, 2048, 512, 256, 512, 512


def setup_inputs():
    n = np.random.standard_normal
    s = mx_kscale(K)[:, None]
    u = mx_kscale(S)
    packed_xT = pack_weight(n((K, T)) * s)
    return {
        "x_words": packed_xT[0],
        "x_scales": packed_xT[1],
        "wa": (n((K, H)) / np.sqrt(K) / s).astype(np.float32),
        "gt": (np.random.uniform(0.5, 1.5, (S, 1)) * u[:, None]).astype(np.float32),
        "w1": (n((S, N)) / np.sqrt(S) / u[:, None]).astype(np.float32),
        "offs": striped(np.random.permutation(T)[:S]),
        "src": striped8(np.stack([np.random.permutation(H)[:V] for _ in range(8)])),
        "dst": striped8(np.stack([np.random.permutation(H)[:V] for _ in range(8)])),
    }


def reference(x_words, x_scales, wa, gt, w1, offs, src, dst):
    xq = unpack_weight(x_words, x_scales)[:, unstriped(offs)]
    y = xq.T @ mxq(f64(wa), 0, "e4m3")
    e = silu(y[np.arange(S)[:, None], runs(src, S)] - (y[np.arange(S)[:, None], runs(dst, S)]))
    d = y.copy()
    d[np.arange(S)[:, None], runs(dst, S)] = e
    z = f64(gt) * d
    return mxq(f64(w1), 0, "e4m3").T @ mxq(z, 0, "e4m3")

@@ -1,0 +1,137 @@
+from contextlib import ExitStack
+
+import concourse.mybir as mybir
+
+K, T, S, V, N, H = 512, 2048, 512, 256, 512, 512
+FLOPS = 2 * S * K * H + 2 * S * N * H
+
+F32 = mybir.dt.float32
+BF16 = mybir.dt.bfloat16
+I32 = mybir.dt.int32
+U32 = mybir.dt.uint32
+U16 = mybir.dt.uint16
+U8 = mybir.dt.uint8
+FP8X4 = mybir.dt.float8_e4m3fn_x4
+ACT = mybir.ActivationFunctionType
+ALU = mybir.AluOpType
+
+P = 128
+PACK = 4
+HALF = 256
+
+
+def weave_views(grouped, raw, c0, c1):
+    dst = grouped.rearrange("p (c i) t -> p c t i", i=4)
+    src = raw[:, :, c0:c1].rearrange("p t (c i) -> p c t i", i=4)
+    return dst, src
+
+
+def tile_picked_featput_silu_p_kernel(tc, x_words, x_scales, wa, gt, w1, offs, src, dst, out):
+    nc = tc.nc
+    with ExitStack() as ctx:
+        keep = ctx.enter_context(tc.tile_pool(name="keep", bufs=1))
+        psum = ctx.enter_context(tc.psum_pool(name="psum", bufs=1))
+
+        offs_sb = keep.tile([P, S // 16], U16, name="offs_sb")
+        src_sb = keep.tile([P, V // 16], U16, name="src_sb")
+        dst_sb = keep.tile([P, V // 16], U16, name="dst_sb")
+        xw = keep.tile([P, T], U32, name="xw")
+        xs = keep.tile([P, T], U8, name="xs")
+        wa_raw = keep.tile([P, PACK, H], F32, name="w_raw")
+        gt_sb = keep.tile([P, PACK], F32, name="gt_sb")
+        warm = keep.tile([P, 2], F32, name="warm")
+
+        nc.vector.memset(xs[:].bitcast(I32), 0)
+        nc.vector.memset(warm[:, 0:1], 0.0)
+        nc.sync.dma_start(offs_sb[:], offs)
+        nc.sync.dma_start(wa_raw[:], wa.rearrange("(p j) n -> p j n", j=PACK))
+        nc.sync.dma_start(xw[:].bitcast(I32), x_words[0].rearrange("p n t -> p (n t)").bitcast(I32))
+        for q in range(4):
+            nc.scalar.dma_start(xs[32 * q : 32 * q + 4, :].bitcast(I32), x_scales[0, 4 * q : 4 * q + 4, :].bitcast(I32))
+        nc.scalar.activation(warm[:, 1:2], warm[:, 0:1], ACT.Silu)
+        nc.sync.dma_start(dst_sb[:], dst)
+        nc.sync.dma_start(src_sb[:], src)
+        nc.gpsimd.dma_start(gt_sb[:], gt.rearrange("(p j) o -> p (j o)", j=PACK))
+
+        gs = keep.tile([P, S], U8, name="gs")
+        xq_s = keep.tile([P, S], U8, name="xq_s", align_bytes=64)
+        xq_w = keep.tile([P, S], U32, name="xq_w", align_bytes=64)
+        nc.vector.tensor_copy(gs[:], xs[:].indirect(offs_sb[:]))
+        nc.vector.tensor_copy(xq_s[:].rearrange("p (t m) -> p t m", t=PACK), gs[:].rearrange("p (m t) -> p t m", t=PACK))
+
+        wa_bf = [keep.tile([P, HALF, PACK], BF16, name="wa_bf%d" % h, align_bytes=64) for h in range(2)]
+        wa_w = [keep.tile([P, HALF], U32, name="wa_w%d" % h, align_bytes=64) for h in range(2)]
+        wa_s = [keep.tile([P, HALF], U8, name="wa_s%d" % h, align_bytes=64) for h in range(2)]
+        d, s = weave_views(wa_bf[0][:], wa_raw, 0, HALF)
+        nc.scalar.copy(d, s)
+        d, s = weave_views(wa_bf[1][:], wa_raw, HALF, H)
+        nc.vector.tensor_copy(d, s)
+        for h in range(2):
+            nc.vector.quantize_mx(wa_w[h][:].bitcast(FP8X4), wa_s[h][:], wa_bf[h][:].rearrange("p n t -> p (n t)"))
+        nc.vector.tensor_copy(xq_w[:].rearrange("p (t m) -> p m t", t=PACK), xw[:].indirect(offs_sb[:]))
+        w1_raw = keep.tile([P, PACK, N], F32, name="w_raw")
+        nc.sync.dma_start(w1_raw[:], w1.rearrange("(p j) n -> p j n", j=PACK))
+
+        y = [keep.tile([P, H], F32, name="y%d" % t) for t in range(PACK)]
+
+        def first_product(t, h):
+            bank = psum.tile([P, HALF], F32, name="bank%d" % (2 * t + h))
+            cols = slice(t * P, (t + 1) * P)
+            nc.tensor.matmul_mx(bank[:], xq_w[:, cols].bitcast(FP8X4), xq_s[:, cols], wa_w[h][:].bitcast(FP8X4), wa_s[h][:], start=True, stop=True)
+            if (t, h) == (0, 1):
+                nc.vector.tensor_copy(y[t][:, h * HALF : (h + 1) * HALF], bank[:])
+            else:
+                nc.scalar.copy(y[t][:, h * HALF : (h + 1) * HALF], bank[:])
+
+        for t, h in ((0, 0), (0, 1), (1, 0), (1, 1), (2, 0), (2, 1), (3, 0), (3, 1)):
+            first_product(t, h)
+
+        g = [keep.tile([P, V], F32, name="g%d" % t) for t in range(PACK)]
+        u = [keep.tile([P, 2, V], F32, name="u%d" % a) for a in range(2)]
+        e = [keep.tile([P, 2, V], F32, name="e%d" % a) for a in range(2)]
+        for a in range(2):
+            for t in (2 * a, 2 * a + 1):
+                nc.vector.tensor_copy(g[t][:], y[t][:].indirect(dst_sb[:]))
+            for t in (2 * a, 2 * a + 1):
+                nc.vector.tensor_tensor(u[a][:, t % 2, :], y[t][:].indirect(src_sb[:]), g[t][:], ALU.subtract)
+            nc.scalar.activation(e[a][:].rearrange("p a v -> p (a v)"), u[a][:].rearrange("p a v -> p (a v)"), ACT.Silu)
+
+        w1_bf = keep.tile([P, N, PACK], BF16, name="w1_bf", align_bytes=64)
+        w1_w = keep.tile([P, N], U32, name="w1_w", align_bytes=64)
+        w1_s = keep.tile([P, N], U8, name="w1_s", align_bytes=64)
+        for m in range(4):
+            d, s = weave_views(w1_bf[:, m * P : (m + 1) * P, :], w1_raw, m * P, (m + 1) * P)
+            nc.scalar.copy(d, s)
+        for h in range(2):
+            cols = slice(h * HALF, (h + 1) * HALF)
+            nc.vector.quantize_mx(w1_w[:, cols].bitcast(FP8X4), w1_s[:, cols], w1_bf[:, cols, :].rearrange("p n t -> p (n t)"))
+
+        z_bf = [keep.tile([P, HALF, PACK], BF16, name="z_bf%d" % h, align_bytes=64) for h in range(2)]
+        z_w = [keep.tile([P, HALF], U32, name="z_w%d" % h, align_bytes=64) for h in range(2)]
+        z_s = [keep.tile([P, HALF], U8, name="z_s%d" % h, align_bytes=64) for h in range(2)]
+        for t in range(PACK):
+            nc.vector.tensor_copy(y[t][:].indirect(dst_sb[:]), e[t // 2][:, t % 2, :])
+            for h in range(2):
+                cols = slice(h * HALF, (h + 1) * HALF)
+                if t < 2 or h == 1:
+                    nc.scalar.activation(z_bf[h][:, :, t], y[t][:, cols], ACT.Copy, scale=gt_sb[:, t : t + 1])
+        for t in (2, 3):
+            nc.vector.tensor_scalar(z_bf[0][:, :, t], y[t][:, 0:HALF], gt_sb[:, t : t + 1], None, ALU.mult)
+        for h in range(2):
+            nc.vector.quantize_mx(z_w[h][:].bitcast(FP8X4), z_s[h][:], z_bf[h][:].rearrange("p n t -> p (n t)"))
+
+        o = [keep.tile([P, H], F32, name="o%d" % m) for m in range(4)]
+
+        def second_product(m, h):
+            bank = psum.tile([P, HALF], F32, name="bank%d" % (2 * m + h))
+            cols = slice(m * P, (m + 1) * P)
+            nc.tensor.matmul_mx(bank[:], w1_w[:, cols].bitcast(FP8X4), w1_s[:, cols], z_w[h][:].bitcast(FP8X4), z_s[h][:], start=True, stop=True)
+            if h == 0:
+                nc.scalar.copy(o[m][:, h * HALF : (h + 1) * HALF], bank[:])
+            else:
+                nc.vector.tensor_copy(o[m][:, h * HALF : (h + 1) * HALF], bank[:])
+
+        for m, h in ((0, 0), (1, 0), (0, 1), (1, 1), (2, 0), (2, 1), (3, 0), (3, 1)):
+            second_product(m, h)
+            if h == 1:
+                nc.sync.dma_start(out[m * P : (m + 1) * P, :], o[m][:])

@@ -38,20 +38,19 @@ def tile_picked_featput_silu_p_kernel(tc, x_words, x_scales, wa, gt, w1, offs, s
         xw = keep.tile([P, T], U32, name="xw")
         xs = keep.tile([P, T], U8, name="xs")
         wa_raw = keep.tile([P, PACK, H], F32, name="w_raw")
-        gt_sb = keep.tile([P, PACK], F32, name="gt_sb")
         warm = keep.tile([P, 2], F32, name="warm")
 
-        nc.vector.memset(xs[:].bitcast(I32), 0)
+        nc.vector.memset(xs[:, 0 : T // 2].bitcast(I32), 0)
+        nc.gpsimd.memset(xs[:, T // 2 : T].bitcast(I32), 0)
         nc.vector.memset(warm[:, 0:1], 0.0)
         nc.sync.dma_start(offs_sb[:], offs)
         nc.sync.dma_start(wa_raw[:], wa.rearrange("(p j) n -> p j n", j=PACK))
-        nc.sync.dma_start(xw[:].bitcast(I32), x_words[0].rearrange("p n t -> p (n t)").bitcast(I32))
+        nc.sync.dma_start(dst_sb[:], dst)
+        nc.sync.dma_start(src_sb[:], src)
         for q in range(4):
             nc.scalar.dma_start(xs[32 * q : 32 * q + 4, :].bitcast(I32), x_scales[0, 4 * q : 4 * q + 4, :].bitcast(I32))
         nc.scalar.activation(warm[:, 1:2], warm[:, 0:1], ACT.Silu)
-        nc.sync.dma_start(dst_sb[:], dst)
-        nc.sync.dma_start(src_sb[:], src)
-        nc.gpsimd.dma_start(gt_sb[:], gt.rearrange("(p j) o -> p (j o)", j=PACK))
+        nc.sync.dma_start(xw[:].bitcast(I32), x_words[0].rearrange("p n t -> p (n t)").bitcast(I32))
 
         gs = keep.tile([P, S], U8, name="gs")
         xq_s = keep.tile([P, S], U8, name="xq_s", align_bytes=64)
@@ -64,13 +63,17 @@ def tile_picked_featput_silu_p_kernel(tc, x_words, x_scales, wa, gt, w1, offs, s
         wa_s = [keep.tile([P, HALF], U8, name="wa_s%d" % h, align_bytes=64) for h in range(2)]
         d, s = weave_views(wa_bf[0][:], wa_raw, 0, HALF)
         nc.scalar.copy(d, s)
-        d, s = weave_views(wa_bf[1][:], wa_raw, HALF, H)
+        d, s = weave_views(wa_bf[1][:, 0:P, :], wa_raw, HALF, HALF + P)
+        nc.scalar.copy(d, s)
+        d, s = weave_views(wa_bf[1][:, P:HALF, :], wa_raw, HALF + P, H)
         nc.vector.tensor_copy(d, s)
         for h in range(2):
             nc.vector.quantize_mx(wa_w[h][:].bitcast(FP8X4), wa_s[h][:], wa_bf[h][:].rearrange("p n t -> p (n t)"))
         nc.vector.tensor_copy(xq_w[:].rearrange("p (t m) -> p m t", t=PACK), xw[:].indirect(offs_sb[:]))
         w1_raw = keep.tile([P, PACK, N], F32, name="w_raw")
         nc.sync.dma_start(w1_raw[:], w1.rearrange("(p j) n -> p j n", j=PACK))
+        gt_sb = keep.tile([P, PACK], F32, name="wa_bf0", align_bytes=64)
+        nc.sync.dma_start(gt_sb[:], gt.rearrange("(p j) o -> p (j o)", j=PACK))
 
         y = [keep.tile([P, H], F32, name="y%d" % t) for t in range(PACK)]
 
@@ -83,55 +86,61 @@ def tile_picked_featput_silu_p_kernel(tc, x_words, x_scales, wa, gt, w1, offs, s
             else:
                 nc.scalar.copy(y[t][:, h * HALF : (h + 1) * HALF], bank[:])
 
-        for t, h in ((0, 0), (0, 1), (1, 0), (1, 1), (2, 0), (2, 1), (3, 0), (3, 1)):
+        for t, h in ((0, 0), (1, 0), (0, 1), (1, 1), (2, 0), (3, 0), (2, 1), (3, 1)):
             first_product(t, h)
 
         g = [keep.tile([P, V], F32, name="g%d" % t) for t in range(PACK)]
-        u = [keep.tile([P, 2, V], F32, name="u%d" % a) for a in range(2)]
-        e = [keep.tile([P, 2, V], F32, name="e%d" % a) for a in range(2)]
+        u = [keep.tile([P, V], F32, name="u%d" % t) for t in range(PACK)]
+        e = [keep.tile([P, V], F32, name="e%d" % t, align_bytes=64) for t in range(PACK)]
         for a in range(2):
             for t in (2 * a, 2 * a + 1):
                 nc.vector.tensor_copy(g[t][:], y[t][:].indirect(dst_sb[:]))
             for t in (2 * a, 2 * a + 1):
-                nc.vector.tensor_tensor(u[a][:, t % 2, :], y[t][:].indirect(src_sb[:]), g[t][:], ALU.subtract)
-            nc.scalar.activation(e[a][:].rearrange("p a v -> p (a v)"), u[a][:].rearrange("p a v -> p (a v)"), ACT.Silu)
+                nc.vector.tensor_tensor(u[t][:], y[t][:].indirect(src_sb[:]), g[t][:], ALU.subtract)
+                nc.scalar.activation(e[t][:], u[t][:], ACT.Silu)
 
         w1_bf = keep.tile([P, N, PACK], BF16, name="w1_bf", align_bytes=64)
-        w1_w = keep.tile([P, N], U32, name="w1_w", align_bytes=64)
-        w1_s = keep.tile([P, N], U8, name="w1_s", align_bytes=64)
+        w1_s = [keep.tile([P, HALF], U8, name="w1_s%d" % h, align_bytes=64) for h in range(2)]
         for m in range(4):
             d, s = weave_views(w1_bf[:, m * P : (m + 1) * P, :], w1_raw, m * P, (m + 1) * P)
             nc.scalar.copy(d, s)
-        for h in range(2):
-            cols = slice(h * HALF, (h + 1) * HALF)
-            nc.vector.quantize_mx(w1_w[:, cols].bitcast(FP8X4), w1_s[:, cols], w1_bf[:, cols, :].rearrange("p n t -> p (n t)"))
 
         z_bf = [keep.tile([P, HALF, PACK], BF16, name="z_bf%d" % h, align_bytes=64) for h in range(2)]
         z_w = [keep.tile([P, HALF], U32, name="z_w%d" % h, align_bytes=64) for h in range(2)]
         z_s = [keep.tile([P, HALF], U8, name="z_s%d" % h, align_bytes=64) for h in range(2)]
         for t in range(PACK):
-            nc.vector.tensor_copy(y[t][:].indirect(dst_sb[:]), e[t // 2][:, t % 2, :])
+            nc.vector.tensor_copy(y[t][:].indirect(dst_sb[:]), e[t][:])
             for h in range(2):
                 cols = slice(h * HALF, (h + 1) * HALF)
                 if t < 2 or h == 1:
                     nc.scalar.activation(z_bf[h][:, :, t], y[t][:, cols], ACT.Copy, scale=gt_sb[:, t : t + 1])
         for t in (2, 3):
             nc.vector.tensor_scalar(z_bf[0][:, :, t], y[t][:, 0:HALF], gt_sb[:, t : t + 1], None, ALU.mult)
+        w1_w = keep.tile([P, N], U32, name="e2", align_bytes=64)
+
+        def quantise_w1(h):
+            cols = slice(h * HALF, (h + 1) * HALF)
+            nc.vector.quantize_mx(w1_w[:, cols].bitcast(FP8X4), w1_s[h][:], w1_bf[:, cols, :].rearrange("p n t -> p (n t)"))
+
+        quantise_w1(0)
         for h in range(2):
             nc.vector.quantize_mx(z_w[h][:].bitcast(FP8X4), z_s[h][:], z_bf[h][:].rearrange("p n t -> p (n t)"))
+        quantise_w1(1)
 
         o = [keep.tile([P, H], F32, name="o%d" % m) for m in range(4)]
 
         def second_product(m, h):
             bank = psum.tile([P, HALF], F32, name="bank%d" % (2 * m + h))
             cols = slice(m * P, (m + 1) * P)
-            nc.tensor.matmul_mx(bank[:], w1_w[:, cols].bitcast(FP8X4), w1_s[:, cols], z_w[h][:].bitcast(FP8X4), z_s[h][:], start=True, stop=True)
+            nc.tensor.matmul_mx(bank[:], w1_w[:, cols].bitcast(FP8X4), w1_s[m // 2][:, (m % 2) * P : (m % 2 + 1) * P], z_w[h][:].bitcast(FP8X4), z_s[h][:], start=True, stop=True)
             if h == 0:
                 nc.scalar.copy(o[m][:, h * HALF : (h + 1) * HALF], bank[:])
             else:
                 nc.vector.tensor_copy(o[m][:, h * HALF : (h + 1) * HALF], bank[:])
 
-        for m, h in ((0, 0), (1, 0), (0, 1), (1, 1), (2, 0), (2, 1), (3, 0), (3, 1)):
+        for m, h in ((0, 0), (0, 1), (1, 0), (1, 1), (2, 0), (2, 1), (3, 0), (3, 1)):
             second_product(m, h)
-            if h == 1:
+            if m in (0, 3):
+                nc.sync.dma_start(out[m * P : (m + 1) * P, h * HALF : (h + 1) * HALF], o[m][:, h * HALF : (h + 1) * HALF])
+            elif h == 1:
                 nc.sync.dma_start(out[m * P : (m + 1) * P, :], o[m][:])

@@ -37,57 +37,71 @@ def tile_picked_featput_silu_p_kernel(tc, x_words, x_scales, wa, gt, w1, offs, s
         dst_sb = keep.tile([P, V // 16], U16, name="dst_sb")
         xw = keep.tile([P, T], U32, name="xw")
         xs = keep.tile([P, T], U8, name="xs")
-        wa_raw = keep.tile([P, PACK, H], F32, name="w_raw")
+        wa_raw = [keep.tile([P, PACK, HALF], F32, name="w_raw%d" % h) for h in range(2)]
         warm = keep.tile([P, 2], F32, name="warm")
 
-        nc.vector.memset(xs[:, 0 : T // 2].bitcast(I32), 0)
-        nc.gpsimd.memset(xs[:, T // 2 : T].bitcast(I32), 0)
+        nc.vector.memset(xs[:, 0 : 3 * T // 4].bitcast(I32), 0)
+        nc.gpsimd.memset(xs[:, 3 * T // 4 : T].bitcast(I32), 0)
         nc.vector.memset(warm[:, 0:1], 0.0)
         nc.sync.dma_start(offs_sb[:], offs)
-        nc.sync.dma_start(wa_raw[:], wa.rearrange("(p j) n -> p j n", j=PACK))
         nc.sync.dma_start(dst_sb[:], dst)
         nc.sync.dma_start(src_sb[:], src)
         for q in range(4):
-            nc.scalar.dma_start(xs[32 * q : 32 * q + 4, :].bitcast(I32), x_scales[0, 4 * q : 4 * q + 4, :].bitcast(I32))
+            nc.sync.dma_start(xs[32 * q : 32 * q + 4, :].bitcast(I32), x_scales[0, 4 * q : 4 * q + 4, :].bitcast(I32))
         nc.scalar.activation(warm[:, 1:2], warm[:, 0:1], ACT.Silu)
         nc.sync.dma_start(xw[:].bitcast(I32), x_words[0].rearrange("p n t -> p (n t)").bitcast(I32))
+        wa_v = wa.rearrange("(p j) n -> p j n", j=PACK)
+        for h in range(2):
+            nc.sync.dma_start(wa_raw[h][:], wa_v[:, :, h * HALF : (h + 1) * HALF])
 
         gs = keep.tile([P, S], U8, name="gs")
         xq_s = keep.tile([P, S], U8, name="xq_s", align_bytes=64)
         xq_w = keep.tile([P, S], U32, name="xq_w", align_bytes=64)
         nc.vector.tensor_copy(gs[:], xs[:].indirect(offs_sb[:]))
         nc.vector.tensor_copy(xq_s[:].rearrange("p (t m) -> p t m", t=PACK), gs[:].rearrange("p (m t) -> p t m", t=PACK))
+        nc.vector.tensor_copy(xq_w[:].rearrange("p (t m) -> p m t", t=PACK), xw[:].indirect(offs_sb[:]))
 
         wa_bf = [keep.tile([P, HALF, PACK], BF16, name="wa_bf%d" % h, align_bytes=64) for h in range(2)]
-        wa_w = [keep.tile([P, HALF], U32, name="wa_w%d" % h, align_bytes=64) for h in range(2)]
-        wa_s = [keep.tile([P, HALF], U8, name="wa_s%d" % h, align_bytes=64) for h in range(2)]
-        d, s = weave_views(wa_bf[0][:], wa_raw, 0, HALF)
-        nc.scalar.copy(d, s)
-        d, s = weave_views(wa_bf[1][:, 0:P, :], wa_raw, HALF, HALF + P)
-        nc.scalar.copy(d, s)
-        d, s = weave_views(wa_bf[1][:, P:HALF, :], wa_raw, HALF + P, H)
-        nc.vector.tensor_copy(d, s)
-        for h in range(2):
-            nc.vector.quantize_mx(wa_w[h][:].bitcast(FP8X4), wa_s[h][:], wa_bf[h][:].rearrange("p n t -> p (n t)"))
-        nc.vector.tensor_copy(xq_w[:].rearrange("p (t m) -> p m t", t=PACK), xw[:].indirect(offs_sb[:]))
-        w1_raw = keep.tile([P, PACK, N], F32, name="w_raw")
+        wa_w = keep.tile([P, H], U32, name="wa_w", align_bytes=64)
+        wa_s = keep.tile([P, H], U8, name="wa_s", align_bytes=64)
+
+        def weave_wa(engine_copy, h, c0, c1):
+            d, s = weave_views(wa_bf[h][:, c0:c1, :], wa_raw[h], c0, c1)
+            engine_copy(d, s)
+
+        def quantise_wa(h, c0, c1):
+            cols = slice(h * HALF + c0, h * HALF + c1)
+            nc.vector.quantize_mx(wa_w[:, cols].bitcast(FP8X4), wa_s[:, cols], wa_bf[h][:, c0:c1, :].rearrange("p n t -> p (n t)"))
+
+        weave_wa(nc.scalar.copy, 0, 0, 96)
+        weave_wa(nc.vector.tensor_copy, 0, 96, HALF)
+        quantise_wa(0, 0, HALF)
+        weave_wa(nc.vector.tensor_copy, 1, 0, P)
+        weave_wa(nc.vector.tensor_copy, 1, P, P + 40)
+        weave_wa(nc.scalar.copy, 1, P + 40, HALF)
+        quantise_wa(1, 0, P)
+        quantise_wa(1, P, HALF)
+        w1_raw = keep.tile([P, PACK, N], F32, name="w_raw0")
         nc.sync.dma_start(w1_raw[:], w1.rearrange("(p j) n -> p j n", j=PACK))
         gt_sb = keep.tile([P, PACK], F32, name="wa_bf0", align_bytes=64)
         nc.sync.dma_start(gt_sb[:], gt.rearrange("(p j) o -> p (j o)", j=PACK))
 
         y = [keep.tile([P, H], F32, name="y%d" % t) for t in range(PACK)]
 
-        def first_product(t, h):
-            bank = psum.tile([P, HALF], F32, name="bank%d" % (2 * t + h))
+        def first_product(b, t, c0, c1, engine_copy):
+            bank = psum.tile([P, c1 - c0], F32, name="bank%d" % b)
             cols = slice(t * P, (t + 1) * P)
-            nc.tensor.matmul_mx(bank[:], xq_w[:, cols].bitcast(FP8X4), xq_s[:, cols], wa_w[h][:].bitcast(FP8X4), wa_s[h][:], start=True, stop=True)
-            if (t, h) == (0, 1):
-                nc.vector.tensor_copy(y[t][:, h * HALF : (h + 1) * HALF], bank[:])
-            else:
-                nc.scalar.copy(y[t][:, h * HALF : (h + 1) * HALF], bank[:])
+            nc.tensor.matmul_mx(bank[:], xq_w[:, cols].bitcast(FP8X4), xq_s[:, cols], wa_w[:, c0:c1].bitcast(FP8X4), wa_s[:, c0:c1], start=True, stop=True)
+            engine_copy(y[t][:, c0:c1], bank[:])
 
-        for t, h in ((0, 0), (1, 0), (0, 1), (1, 1), (2, 0), (3, 0), (2, 1), (3, 1)):
-            first_product(t, h)
+        first_product(0, 0, 0, HALF, nc.scalar.copy)
+        first_product(1, 1, 0, HALF, nc.scalar.copy)
+        first_product(2, 0, HALF, HALF + P, nc.scalar.copy)
+        first_product(3, 1, HALF, HALF + P, nc.scalar.copy)
+        first_product(4, 0, HALF + P, H, nc.vector.tensor_copy)
+        first_product(5, 1, HALF + P, H, nc.scalar.copy)
+        first_product(6, 2, 0, H, nc.scalar.copy)
+        first_product(7, 3, 0, H, nc.scalar.copy)
 
         g = [keep.tile([P, V], F32, name="g%d" % t) for t in range(PACK)]
         u = [keep.tile([P, V], F32, name="u%d" % t) for t in range(PACK)]

@@ -37,7 +37,7 @@ def tile_picked_featput_silu_p_kernel(tc, x_words, x_scales, wa, gt, w1, offs, s
         dst_sb = keep.tile([P, V // 16], U16, name="dst_sb")
         xw = keep.tile([P, T], U32, name="xw")
         xs = keep.tile([P, T], U8, name="xs")
-        wa_raw = [keep.tile([P, PACK, HALF], F32, name="w_raw%d" % h) for h in range(2)]
+        wa_raw = [keep.tile([P, PACK, HALF], F32, name="w_raw%d" % h, align_bytes=64) for h in range(2)]
         warm = keep.tile([P, 2], F32, name="warm")
 
         nc.vector.memset(xs[:, 0 : 3 * T // 4].bitcast(I32), 0)
@@ -81,12 +81,12 @@ def tile_picked_featput_silu_p_kernel(tc, x_words, x_scales, wa, gt, w1, offs, s
         weave_wa(nc.scalar.copy, 1, P + 40, HALF)
         quantise_wa(1, 0, P)
         quantise_wa(1, P, HALF)
-        w1_raw = keep.tile([P, PACK, N], F32, name="w_raw0")
+        w1_raw = keep.tile([P, PACK, N], F32, name="w_raw0", align_bytes=64)
         nc.sync.dma_start(w1_raw[:], w1.rearrange("(p j) n -> p j n", j=PACK))
         gt_sb = keep.tile([P, PACK], F32, name="wa_bf0", align_bytes=64)
         nc.sync.dma_start(gt_sb[:], gt.rearrange("(p j) o -> p (j o)", j=PACK))
 
-        y = [keep.tile([P, H], F32, name="y%d" % t) for t in range(PACK)]
+        y = [keep.tile([P, H], F32, name="y%d" % t, align_bytes=64) for t in range(PACK)]
 
         def first_product(b, t, c0, c1, engine_copy):
             bank = psum.tile([P, c1 - c0], F32, name="bank%d" % b)
@@ -100,12 +100,14 @@ def tile_picked_featput_silu_p_kernel(tc, x_words, x_scales, wa, gt, w1, offs, s
         first_product(3, 1, HALF, HALF + P, nc.scalar.copy)
         first_product(4, 0, HALF + P, H, nc.vector.tensor_copy)
         first_product(5, 1, HALF + P, H, nc.scalar.copy)
-        first_product(6, 2, 0, H, nc.scalar.copy)
-        first_product(7, 3, 0, H, nc.scalar.copy)
+        first_product(6, 2, HALF, H, nc.scalar.copy)
+        first_product(7, 3, HALF, H, nc.scalar.copy)
+        first_product(2, 2, 0, HALF, nc.scalar.copy)
+        first_product(3, 3, 0, HALF, nc.scalar.copy)
 
         g = [keep.tile([P, V], F32, name="g%d" % t) for t in range(PACK)]
         u = [keep.tile([P, V], F32, name="u%d" % t) for t in range(PACK)]
-        e = [keep.tile([P, V], F32, name="e%d" % t, align_bytes=64) for t in range(PACK)]
+        e = [keep.tile([P, V], F32, name=("wa_s", "e1", "e2", "e3")[t], align_bytes=64) for t in range(PACK)]
         for a in range(2):
             for t in (2 * a, 2 * a + 1):
                 nc.vector.tensor_copy(g[t][:], y[t][:].indirect(dst_sb[:]))
@@ -114,47 +116,59 @@ def tile_picked_featput_silu_p_kernel(tc, x_words, x_scales, wa, gt, w1, offs, s
                 nc.scalar.activation(e[t][:], u[t][:], ACT.Silu)
 
         w1_bf = keep.tile([P, N, PACK], BF16, name="w1_bf", align_bytes=64)
-        w1_s = [keep.tile([P, HALF], U8, name="w1_s%d" % h, align_bytes=64) for h in range(2)]
         for m in range(4):
             d, s = weave_views(w1_bf[:, m * P : (m + 1) * P, :], w1_raw, m * P, (m + 1) * P)
             nc.scalar.copy(d, s)
 
-        z_bf = [keep.tile([P, HALF, PACK], BF16, name="z_bf%d" % h, align_bytes=64) for h in range(2)]
-        z_w = [keep.tile([P, HALF], U32, name="z_w%d" % h, align_bytes=64) for h in range(2)]
-        z_s = [keep.tile([P, HALF], U8, name="z_s%d" % h, align_bytes=64) for h in range(2)]
+        z_bf = keep.tile([P, H, PACK], BF16, name="w_raw0", align_bytes=64)
+        z_w = keep.tile([P, H], U32, name="z_w", align_bytes=64)
+        z_s = keep.tile([P, H], U8, name="z_s", align_bytes=64)
+        w1_s = keep.tile([P, N], U8, name="w1_s", align_bytes=64)
         for t in range(PACK):
             nc.vector.tensor_copy(y[t][:].indirect(dst_sb[:]), e[t][:])
-            for h in range(2):
-                cols = slice(h * HALF, (h + 1) * HALF)
-                if t < 2 or h == 1:
-                    nc.scalar.activation(z_bf[h][:, :, t], y[t][:, cols], ACT.Copy, scale=gt_sb[:, t : t + 1])
+            c0 = 0 if t < 2 else HALF
+            nc.scalar.activation(z_bf[:, c0:H, t], y[t][:, c0:H], ACT.Copy, scale=gt_sb[:, t : t + 1])
         for t in (2, 3):
-            nc.vector.tensor_scalar(z_bf[0][:, :, t], y[t][:, 0:HALF], gt_sb[:, t : t + 1], None, ALU.mult)
-        w1_w = keep.tile([P, N], U32, name="e2", align_bytes=64)
+            nc.vector.tensor_scalar(z_bf[:, 0:HALF, t], y[t][:, 0:HALF], gt_sb[:, t : t + 1], None, ALU.mult)
 
-        def quantise_w1(h):
+        def quantise_w1(tag, c0, c1):
+            words = keep.tile([P, c1 - c0], U32, name=tag, align_bytes=64)
+            nc.vector.quantize_mx(words[:].bitcast(FP8X4), w1_s[:, c0:c1], w1_bf[:, c0:c1, :].rearrange("p n t -> p (n t)"))
+            return [words[:, c : c + P] for c in range(0, c1 - c0, P)]
+
+        def quantise_z(h):
             cols = slice(h * HALF, (h + 1) * HALF)
-            nc.vector.quantize_mx(w1_w[:, cols].bitcast(FP8X4), w1_s[h][:], w1_bf[:, cols, :].rearrange("p n t -> p (n t)"))
+            nc.vector.quantize_mx(z_w[:, cols].bitcast(FP8X4), z_s[:, cols], z_bf[:, cols, :].rearrange("p n t -> p (n t)"))
 
-        quantise_w1(0)
-        for h in range(2):
-            nc.vector.quantize_mx(z_w[h][:].bitcast(FP8X4), z_s[h][:], z_bf[h][:].rearrange("p n t -> p (n t)"))
-        quantise_w1(1)
+        w1_w = quantise_w1("e2", 0, P)
+        quantise_z(0)
+        w1_w = w1_w + quantise_w1("y1", P, HALF)
+        quantise_z(1)
+        w1_w = w1_w + quantise_w1("y3", HALF, N)
 
         o = [keep.tile([P, H], F32, name="o%d" % m) for m in range(4)]
 
-        def second_product(m, h):
+        def second_product(m, h, engine_copy):
             bank = psum.tile([P, HALF], F32, name="bank%d" % (2 * m + h))
-            cols = slice(m * P, (m + 1) * P)
-            nc.tensor.matmul_mx(bank[:], w1_w[:, cols].bitcast(FP8X4), w1_s[m // 2][:, (m % 2) * P : (m % 2 + 1) * P], z_w[h][:].bitcast(FP8X4), z_s[h][:], start=True, stop=True)
-            if h == 0:
-                nc.scalar.copy(o[m][:, h * HALF : (h + 1) * HALF], bank[:])
-            else:
-                nc.vector.tensor_copy(o[m][:, h * HALF : (h + 1) * HALF], bank[:])
+            cols = slice(h * HALF, (h + 1) * HALF)
+            nc.tensor.matmul_mx(bank[:], w1_w[m].bitcast(FP8X4), w1_s[:, m * P : (m + 1) * P], z_w[:, cols].bitcast(FP8X4), z_s[:, cols], start=True, stop=True)
+            engine_copy(o[m][:, cols], bank[:])
 
-        for m, h in ((0, 0), (0, 1), (1, 0), (1, 1), (2, 0), (2, 1), (3, 0), (3, 1)):
-            second_product(m, h)
-            if m in (0, 3):
-                nc.sync.dma_start(out[m * P : (m + 1) * P, h * HALF : (h + 1) * HALF], o[m][:, h * HALF : (h + 1) * HALF])
-            elif h == 1:
-                nc.sync.dma_start(out[m * P : (m + 1) * P, :], o[m][:])
+        def store(m, c0, c1):
+            nc.sync.dma_start(out[m * P : (m + 1) * P, c0:c1], o[m][:, c0:c1])
+
+        second_product(0, 0, nc.scalar.copy)
+        store(0, 0, HALF)
+        second_product(1, 0, nc.scalar.copy)
+        store(1, 0, HALF)
+        second_product(0, 1, nc.scalar.copy)
+        store(0, HALF, H)
+        second_product(1, 1, nc.vector.tensor_copy)
+        store(1, HALF, H)
+        second_product(2, 0, nc.scalar.copy)
+        second_product(2, 1, nc.vector.tensor_copy)
+        store(2, 0, H)
+        second_product(3, 0, nc.scalar.copy)
+        store(3, 0, HALF)
+        second_product(3, 1, nc.vector.tensor_copy)
+        store(3, HALF, H)

@@ -38,21 +38,20 @@ def tile_picked_featput_silu_p_kernel(tc, x_words, x_scales, wa, gt, w1, offs, s
         xw = keep.tile([P, T], U32, name="xw")
         xs = keep.tile([P, T], U8, name="xs")
         wa_raw = [keep.tile([P, PACK, HALF], F32, name="w_raw%d" % h, align_bytes=64) for h in range(2)]
-        warm = keep.tile([P, 2], F32, name="warm")
 
         nc.vector.memset(xs[:, 0 : 3 * T // 4].bitcast(I32), 0)
         nc.gpsimd.memset(xs[:, 3 * T // 4 : T].bitcast(I32), 0)
-        nc.vector.memset(warm[:, 0:1], 0.0)
         nc.sync.dma_start(offs_sb[:], offs)
+        x_v = x_words[0].rearrange("p n t -> p (n t)").bitcast(I32)
+        nc.sync.dma_start(xw[:, 0:512].bitcast(I32), x_v[:, 0:512])
         nc.sync.dma_start(dst_sb[:], dst)
-        nc.sync.dma_start(src_sb[:], src)
         for q in range(4):
             nc.sync.dma_start(xs[32 * q : 32 * q + 4, :].bitcast(I32), x_scales[0, 4 * q : 4 * q + 4, :].bitcast(I32))
-        nc.scalar.activation(warm[:, 1:2], warm[:, 0:1], ACT.Silu)
-        nc.sync.dma_start(xw[:].bitcast(I32), x_words[0].rearrange("p n t -> p (n t)").bitcast(I32))
+        nc.sync.dma_start(xw[:, 512:T].bitcast(I32), x_v[:, 512:T])
         wa_v = wa.rearrange("(p j) n -> p j n", j=PACK)
         for h in range(2):
             nc.sync.dma_start(wa_raw[h][:], wa_v[:, :, h * HALF : (h + 1) * HALF])
+        nc.sync.dma_start(src_sb[:], src)
 
         gs = keep.tile([P, S], U8, name="gs")
         xq_s = keep.tile([P, S], U8, name="xq_s", align_bytes=64)
@@ -73,8 +72,7 @@ def tile_picked_featput_silu_p_kernel(tc, x_words, x_scales, wa, gt, w1, offs, s
             cols = slice(h * HALF + c0, h * HALF + c1)
             nc.vector.quantize_mx(wa_w[:, cols].bitcast(FP8X4), wa_s[:, cols], wa_bf[h][:, c0:c1, :].rearrange("p n t -> p (n t)"))
 
-        weave_wa(nc.scalar.copy, 0, 0, 96)
-        weave_wa(nc.vector.tensor_copy, 0, 96, HALF)
+        weave_wa(nc.vector.tensor_copy, 0, 0, HALF)
         quantise_wa(0, 0, HALF)
         weave_wa(nc.vector.tensor_copy, 1, 0, P)
         weave_wa(nc.vector.tensor_copy, 1, P, P + 40)
@@ -116,8 +114,8 @@ def tile_picked_featput_silu_p_kernel(tc, x_words, x_scales, wa, gt, w1, offs, s
                 nc.scalar.activation(e[t][:], u[t][:], ACT.Silu)
 
         w1_bf = keep.tile([P, N, PACK], BF16, name="w1_bf", align_bytes=64)
-        for m in range(4):
-            d, s = weave_views(w1_bf[:, m * P : (m + 1) * P, :], w1_raw, m * P, (m + 1) * P)
+        for h in range(2):
+            d, s = weave_views(w1_bf[:, h * HALF : (h + 1) * HALF, :], w1_raw, h * HALF, (h + 1) * HALF)
             nc.scalar.copy(d, s)
 
         z_bf = keep.tile([P, H, PACK], BF16, name="w_raw0", align_bytes=64)

from contextlib import ExitStack

import concourse.mybir as mybir

K, T, S, V, N, H = 512, 2048, 512, 256, 512, 512
FLOPS = 2 * S * K * H + 2 * S * N * H

F32 = mybir.dt.float32
BF16 = mybir.dt.bfloat16
I32 = mybir.dt.int32
U32 = mybir.dt.uint32
U16 = mybir.dt.uint16
U8 = mybir.dt.uint8
FP8X4 = mybir.dt.float8_e4m3fn_x4
ACT = mybir.ActivationFunctionType
ALU = mybir.AluOpType

P = 128
PACK = 4
HALF = 256


def weave_views(grouped, raw, c0, c1):
    dst = grouped.rearrange("p (c i) t -> p c t i", i=4)
    src = raw[:, :, c0:c1].rearrange("p t (c i) -> p c t i", i=4)
    return dst, src


def tile_picked_featput_silu_p_kernel(tc, x_words, x_scales, wa, gt, w1, offs, src, dst, out):
    nc = tc.nc
    with ExitStack() as ctx:
        keep = ctx.enter_context(tc.tile_pool(name="keep", bufs=1))
        psum = ctx.enter_context(tc.psum_pool(name="psum", bufs=1))

        offs_sb = keep.tile([P, S // 16], U16, name="offs_sb")
        src_sb = keep.tile([P, V // 16], U16, name="src_sb")
        dst_sb = keep.tile([P, V // 16], U16, name="dst_sb")
        xw = keep.tile([P, T], U32, name="xw")
        xs = keep.tile([P, T], U8, name="xs")
        wa_raw = [keep.tile([P, PACK, HALF], F32, name="w_raw%d" % h, align_bytes=64) for h in range(2)]

        nc.vector.memset(xs[:, 0 : 3 * T // 4].bitcast(I32), 0)
        nc.gpsimd.memset(xs[:, 3 * T // 4 : T].bitcast(I32), 0)
        nc.sync.dma_start(offs_sb[:], offs)
        x_v = x_words[0].rearrange("p n t -> p (n t)").bitcast(I32)
        nc.sync.dma_start(xw[:, 0:512].bitcast(I32), x_v[:, 0:512])
        nc.sync.dma_start(dst_sb[:], dst)
        for q in range(4):
            nc.sync.dma_start(xs[32 * q : 32 * q + 4, :].bitcast(I32), x_scales[0, 4 * q : 4 * q + 4, :].bitcast(I32))
        nc.sync.dma_start(xw[:, 512:T].bitcast(I32), x_v[:, 512:T])
        wa_v = wa.rearrange("(p j) n -> p j n", j=PACK)
        for h in range(2):
            nc.sync.dma_start(wa_raw[h][:], wa_v[:, :, h * HALF : (h + 1) * HALF])
        nc.sync.dma_start(src_sb[:], src)

        gs = keep.tile([P, S], U8, name="gs")
        xq_s = keep.tile([P, S], U8, name="xq_s", align_bytes=64)
        xq_w = keep.tile([P, S], U32, name="xq_w", align_bytes=64)
        nc.vector.tensor_copy(gs[:], xs[:].indirect(offs_sb[:]))
        nc.vector.tensor_copy(xq_s[:].rearrange("p (t m) -> p t m", t=PACK), gs[:].rearrange("p (m t) -> p t m", t=PACK))
        nc.vector.tensor_copy(xq_w[:].rearrange("p (t m) -> p m t", t=PACK), xw[:].indirect(offs_sb[:]))

        wa_bf = [keep.tile([P, HALF, PACK], BF16, name="wa_bf%d" % h, align_bytes=64) for h in range(2)]
        wa_w = keep.tile([P, H], U32, name="wa_w", align_bytes=64)
        wa_s = keep.tile([P, H], U8, name="wa_s", align_bytes=64)

        def weave_wa(engine_copy, h, c0, c1):
            d, s = weave_views(wa_bf[h][:, c0:c1, :], wa_raw[h], c0, c1)
            engine_copy(d, s)

        def quantise_wa(h, c0, c1):
            cols = slice(h * HALF + c0, h * HALF + c1)
            nc.vector.quantize_mx(wa_w[:, cols].bitcast(FP8X4), wa_s[:, cols], wa_bf[h][:, c0:c1, :].rearrange("p n t -> p (n t)"))

        weave_wa(nc.vector.tensor_copy, 0, 0, HALF)
        quantise_wa(0, 0, HALF)
        weave_wa(nc.vector.tensor_copy, 1, 0, P)
        weave_wa(nc.vector.tensor_copy, 1, P, P + 40)
        weave_wa(nc.scalar.copy, 1, P + 40, HALF)
        quantise_wa(1, 0, P)
        quantise_wa(1, P, HALF)
        w1_raw = keep.tile([P, PACK, N], F32, name="w_raw0", align_bytes=64)
        nc.sync.dma_start(w1_raw[:], w1.rearrange("(p j) n -> p j n", j=PACK))
        gt_sb = keep.tile([P, PACK], F32, name="wa_bf0", align_bytes=64)
        nc.sync.dma_start(gt_sb[:], gt.rearrange("(p j) o -> p (j o)", j=PACK))

        y = [keep.tile([P, H], F32, name="y%d" % t, align_bytes=64) for t in range(PACK)]

        def first_product(b, t, c0, c1, engine_copy):
            bank = psum.tile([P, c1 - c0], F32, name="bank%d" % b)
            cols = slice(t * P, (t + 1) * P)
            nc.tensor.matmul_mx(bank[:], xq_w[:, cols].bitcast(FP8X4), xq_s[:, cols], wa_w[:, c0:c1].bitcast(FP8X4), wa_s[:, c0:c1], start=True, stop=True)
            engine_copy(y[t][:, c0:c1], bank[:])

        first_product(0, 0, 0, HALF, nc.scalar.copy)
        first_product(1, 1, 0, HALF, nc.scalar.copy)
        first_product(2, 0, HALF, HALF + P, nc.scalar.copy)
        first_product(3, 1, HALF, HALF + P, nc.scalar.copy)
        first_product(4, 0, HALF + P, H, nc.vector.tensor_copy)
        first_product(5, 1, HALF + P, H, nc.scalar.copy)
        first_product(6, 2, HALF, H, nc.scalar.copy)
        first_product(7, 3, HALF, H, nc.scalar.copy)
        first_product(2, 2, 0, HALF, nc.scalar.copy)
        first_product(3, 3, 0, HALF, nc.scalar.copy)

        g = [keep.tile([P, V], F32, name="g%d" % t) for t in range(PACK)]
        u = [keep.tile([P, V], F32, name="u%d" % t) for t in range(PACK)]
        e = [keep.tile([P, V], F32, name=("wa_s", "e1", "e2", "e3")[t], align_bytes=64) for t in range(PACK)]
        for a in range(2):
            for t in (2 * a, 2 * a + 1):
                nc.vector.tensor_copy(g[t][:], y[t][:].indirect(dst_sb[:]))
            for t in (2 * a, 2 * a + 1):
                nc.vector.tensor_tensor(u[t][:], y[t][:].indirect(src_sb[:]), g[t][:], ALU.subtract)
                nc.scalar.activation(e[t][:], u[t][:], ACT.Silu)

        w1_bf = keep.tile([P, N, PACK], BF16, name="w1_bf", align_bytes=64)
        for h in range(2):
            d, s = weave_views(w1_bf[:, h * HALF : (h + 1) * HALF, :], w1_raw, h * HALF, (h + 1) * HALF)
            nc.scalar.copy(d, s)

        z_bf = keep.tile([P, H, PACK], BF16, name="w_raw0", align_bytes=64)
        z_w = keep.tile([P, H], U32, name="z_w", align_bytes=64)
        z_s = keep.tile([P, H], U8, name="z_s", align_bytes=64)
        w1_s = keep.tile([P, N], U8, name="w1_s", align_bytes=64)
        for t in range(PACK):
            nc.vector.tensor_copy(y[t][:].indirect(dst_sb[:]), e[t][:])
            c0 = 0 if t < 2 else HALF
            nc.scalar.activation(z_bf[:, c0:H, t], y[t][:, c0:H], ACT.Copy, scale=gt_sb[:, t : t + 1])
        for t in (2, 3):
            nc.vector.tensor_scalar(z_bf[:, 0:HALF, t], y[t][:, 0:HALF], gt_sb[:, t : t + 1], None, ALU.mult)

        def quantise_w1(tag, c0, c1):
            words = keep.tile([P, c1 - c0], U32, name=tag, align_bytes=64)
            nc.vector.quantize_mx(words[:].bitcast(FP8X4), w1_s[:, c0:c1], w1_bf[:, c0:c1, :].rearrange("p n t -> p (n t)"))
            return [words[:, c : c + P] for c in range(0, c1 - c0, P)]

        def quantise_z(h):
            cols = slice(h * HALF, (h + 1) * HALF)
            nc.vector.quantize_mx(z_w[:, cols].bitcast(FP8X4), z_s[:, cols], z_bf[:, cols, :].rearrange("p n t -> p (n t)"))

        w1_w = quantise_w1("e2", 0, P)
        quantise_z(0)
        w1_w = w1_w + quantise_w1("y1", P, HALF)
        quantise_z(1)
        w1_w = w1_w + quantise_w1("y3", HALF, N)

        o = [keep.tile([P, H], F32, name="o%d" % m) for m in range(4)]

        def second_product(m, h, engine_copy):
            bank = psum.tile([P, HALF], F32, name="bank%d" % (2 * m + h))
            cols = slice(h * HALF, (h + 1) * HALF)
            nc.tensor.matmul_mx(bank[:], w1_w[m].bitcast(FP8X4), w1_s[:, m * P : (m + 1) * P], z_w[:, cols].bitcast(FP8X4), z_s[:, cols], start=True, stop=True)
            engine_copy(o[m][:, cols], bank[:])

        def store(m, c0, c1):
            nc.sync.dma_start(out[m * P : (m + 1) * P, c0:c1], o[m][:, c0:c1])

        second_product(0, 0, nc.scalar.copy)
        store(0, 0, HALF)
        second_product(1, 0, nc.scalar.copy)
        store(1, 0, HALF)
        second_product(0, 1, nc.scalar.copy)
        store(0, HALF, H)
        second_product(1, 1, nc.vector.tensor_copy)
        store(1, HALF, H)
        second_product(2, 0, nc.scalar.copy)
        second_product(2, 1, nc.vector.tensor_copy)
        store(2, 0, H)
        second_product(3, 0, nc.scalar.copy)
        store(3, 0, HALF)
        second_product(3, 1, nc.vector.tensor_copy)
        store(3, HALF, H)
